import numpy as np
import ml_dtypes


def mxq(x, axis, fmt="e4m3"):
    dtype, down = {"e4m3": (ml_dtypes.float8_e4m3fn, 7), "e5m2": (ml_dtypes.float8_e5m2, 14)}[fmt]
    v = np.moveaxis(np.asarray(x, np.float32).astype(ml_dtypes.bfloat16).astype(np.float64), axis, -1)
    blocks = v.reshape(v.shape[:-1] + (-1, 32))
    amax = np.abs(blocks).max(-1, keepdims=True)
    byte = np.maximum(np.where(amax > 0, np.frexp(amax)[1] - 1 + 127, 0) - down, 1)
    scale = np.exp2(byte - 127.0)
    codes = (blocks / scale).astype(np.float32).astype(dtype).astype(np.float64)
    return np.moveaxis((codes * scale).reshape(v.shape), -1, axis)


WIDE = False


def mx_kscale(k):
    if not WIDE:
        return np.ones(k)
    levels = np.array([10, -10, 5, -5, 0])
    if k % 512:
        return np.exp2(np.random.permutation(np.resize(levels, k // 32))).repeat(32)
    a = np.empty((k // 512, 16))
    for p in range(k // 512):
        a[p, :8] = np.random.permutation(np.resize(levels, 8))
        for g in range(8):
            far = levels[np.abs(levels - a[p, g]) >= 10]
            a[p, g + 8] = far[np.random.randint(len(far))]
    return np.exp2(a.ravel()).repeat(32)


def f64(x):
    return np.asarray(x).astype(np.float64)


def striped(idx):
    return np.tile(np.asarray(idx).reshape(-1, 16).T, (8, 1)).astype(np.uint16)


def unstriped(offs):
    return offs[:16].T.reshape(-1).astype(np.int64)


E2M1 = np.array([0.0, 0.5, 1.0, 1.5, 2.0, 3.0, 4.0, 6.0, -0.0, -0.5, -1.0, -1.5, -2.0, -3.0, -4.0, -6.0])


def pack_weight(w, fmt):
    k, n = w.shape
    w = f64(np.asarray(w, np.float32).astype(ml_dtypes.bfloat16)).reshape(k // 32, 32, n)
    amax = np.abs(w).max(1)
    if fmt == "e4m3":
        byte = np.frexp(amax)[1] - 1 + 127 - 7
    else:
        mant, ex = np.frexp(amax / 6.0)
        byte = np.where(mant > 0.5, ex, ex - 1) + 127
    byte = np.clip(np.where(amax > 0, byte, 1), 1, 254)
    scaled = (w * np.exp2(127.0 - byte)[:, None, :]).reshape(k, n).astype(np.float32)
    by_word = np.ascontiguousarray(scaled.reshape(k // 512, 128, 4, n).transpose(0, 1, 3, 2))
    if fmt == "e4m3":
        words = by_word.astype(ml_dtypes.float8_e4m3fn).view(np.uint8)
    else:
        c = by_word.astype(ml_dtypes.float4_e2m1fn).view(np.uint8) & 0xF
        words = (c[..., 0::2] | (c[..., 1::2] << 4)).reshape(k // 512, 128, 2 * n)
    return np.ascontiguousarray(words), np.ascontiguousarray(byte.astype(np.uint8).reshape(k // 512, 16, n))


def unpack_weight(words, scales, fmt):
    g, _, n = scales.shape
    words = np.ascontiguousarray(words).reshape(g, 128, n, -1)
    if fmt == "e4m3":
        vals = words.view(ml_dtypes.float8_e4m3fn).astype(np.float64)
    else:
        nib = np.empty((g, 128, n, 4), np.uint8)
        nib[..., 0::2] = words & 0xF
        nib[..., 1::2] = words >> 4
        vals = E2M1[nib]
    vals = vals * np.repeat(np.exp2(scales.astype(np.float64) - 127.0), 8, axis=1)[..., None]
    return vals.transpose(0, 1, 3, 2).reshape(g * 512, n)


def sigmoid(v):
    return 1.0 / (1.0 + np.exp(-v))


D, T, I, Q, E = 512, 2048, 512, 128, 512


def setup_inputs():
    n = np.random.standard_normal
    idx = np.random.permutation(T)[:I]
    fd = mx_kscale(D)
    fi = mx_kscale(I)
    ti = np.ones(T)
    ti[idx] = fi
    keysp = pack_weight(n((D, T)) / fd[:, None], "e2m1")
    return {
        "query": (n((D, Q)) * 0.9 / np.sqrt(D) * fd[:, None]).astype(np.float32),
        "keys_words": keysp[0],
        "keys_scales": keysp[1],
        "th": (np.random.uniform(5.6, 6.1, (Q, 1))).astype(np.float32),
        "steep": (np.random.uniform(1.0, 5.0, (Q, 1))).astype(np.float32),
        "stand": (0.1 * n((1, E))).astype(np.float32),
        "size": (np.random.uniform(0.5, 2.0, (1, I)) * fi).astype(np.float32),
        "vals": (n((E, T)) / ti).astype(np.float32),
        "offs": striped(idx),
    }


def reference(query, keys_words, keys_scales, th, steep, stand, size, vals, offs):
    idx = unstriped(offs)
    keysu = unpack_weight(keys_words, keys_scales, "e2m1")
    queryq = mxq(f64(query), 0, "e4m3")
    keysidxg = keysu[:, idx]
    a = queryq.T @ keysidxg
    b = a - np.max(a, axis=1, keepdims=True)
    p = np.exp(b)
    z = np.sum(p, axis=1, keepdims=True)
    en = np.log(z) - np.sum(p * b, axis=1, keepdims=True) / z
    g = sigmoid((f64(th) - en) * f64(steep))
    w = p * f64(size) / z
    wt = w.T
    vt = f64(vals)[:, idx].T
    wtq = mxq(wt, 0, "e4m3")
    vtq = mxq(vt, 0, "e4m3")
    o = wtq.T @ vtq
    y = f64(stand) + (o - f64(stand)) * g
    return y

@@ -1,0 +1,186 @@
+import math
+from contextlib import ExitStack
+
+import concourse.mybir as mybir
+from concourse.masks import make_identity
+
+D, T, I, Q, E = 512, 2048, 512, 128, 512
+FLOPS = 2 * Q * D * I + 2 * Q * I * E
+
+F32 = mybir.dt.float32
+BF16 = mybir.dt.bfloat16
+I32 = mybir.dt.int32
+U32 = mybir.dt.uint32
+U16 = mybir.dt.uint16
+U8 = mybir.dt.uint8
+FP8X4 = mybir.dt.float8_e4m3fn_x4
+FP4X4 = mybir.dt.float4_e2m1fn_x4
+ALU = mybir.AluOpType
+ACT = mybir.ActivationFunctionType
+
+P = 128
+PACK = 4
+BLOCKS = E // P
+SPLIT = 288
+EN_MAX = math.log(I)
+
+
+def tile_attend_certaintyread_kernel(tc, query, keys_words, keys_scales, th, steep, stand, size, vals, offs, out):
+    nc = tc.nc
+    with ExitStack() as ctx:
+        sb = ctx.enter_context(tc.tile_pool(name="sb", bufs=1))
+        ps = ctx.enter_context(tc.psum_pool(name="ps", bufs=1))
+
+        offsets = sb.tile([P, I // 16], U16, name="offsets")
+        key_words = sb.tile([P, T], U16, name="key_words", align_bytes=64)
+        key_bytes = sb.tile([P, T], U8, name="key_bytes", align_bytes=64)
+        ident = sb.tile([P, P], F32, name="ident")
+
+        nc.vector.memset(key_bytes[:].bitcast(I32), 0)
+        make_identity(nc, ident[:])
+
+        def load_pool(j):
+            pool = sb.tile([P, T], F32, name="pool%d" % j, tag="pool%d" % j, align_bytes=64)
+            nc.sync.dma_start(pool[:], vals[j * P : (j + 1) * P, :])
+            return pool
+
+        size4 = sb.tile([P, PACK], F32, name="size4")
+        stand4 = sb.tile([P, PACK], F32, name="stand4")
+        th_col = sb.tile([P, 1], F32, name="th_col")
+        steep_col = sb.tile([P, 1], F32, name="steep_col")
+        q_raw = sb.tile([P, PACK, Q], F32, name="q_raw", align_bytes=64)
+        nc.sync.dma_start(offsets[:], offs)
+        nc.sync.dma_start(key_words[:].bitcast(I32), keys_words[0].bitcast(I32))
+        nc.sync.dma_start(size4[:], size.rearrange("o (p j) -> p (o j)", j=PACK))
+        for quad in range(4):
+            nc.sync.dma_start(
+                key_bytes[32 * quad : 32 * quad + 4, :].bitcast(I32),
+                keys_scales[0, 4 * quad : 4 * quad + 4, :].bitcast(I32),
+            )
+        nc.sync.dma_start(q_raw[:], query.rearrange("(p j) q -> p j q", j=PACK))
+        pools = [load_pool(0)]
+        with nc.allow_non_contiguous_dma(reason="one value a partition"):
+            nc.sync.dma_start(th_col[:], th)
+            nc.sync.dma_start(steep_col[:], steep)
+        nc.sync.dma_start(stand4[:], stand.rearrange("o (p j) -> p (o j)", j=PACK))
+        pools.extend(load_pool(j) for j in range(1, BLOCKS))
+
+        got_words = sb.tile([P, I], U16, name="got_words", align_bytes=64)
+        got_bytes = sb.tile([P, I], U8, name="got_bytes", align_bytes=64)
+        nc.vector.tensor_copy(got_words[:], key_words[:].indirect(offsets[:]))
+        nc.vector.tensor_copy(got_bytes[:], key_bytes[:].indirect(offsets[:]))
+
+        q_bf = sb.tile([P, Q * PACK], BF16, name="q_bf", align_bytes=64)
+        nc.scalar.copy(q_bf[:].rearrange("p (q j) -> p q j", j=PACK), q_raw[:].rearrange("p j q -> p q j"))
+        q_codes = sb.tile([P, Q], U32, name="q_codes", align_bytes=64)
+        q_plane = sb.tile([P, Q], U8, name="q_plane", align_bytes=64)
+        nc.vector.quantize_mx(out=q_codes[:].bitcast(FP8X4), scales=q_plane[:], in_=q_bf[:])
+
+        scores = ps.tile([P, I], F32, name="scores", tag="scores")
+        nc.tensor.matmul_mx(
+            out=scores[:], lhsT=q_codes[:].bitcast(FP8X4), lhsT_scale=q_plane[:],
+            rhs=got_words[:].bitcast(FP4X4), rhs_scale=got_bytes[:], start=True, stop=True,
+        )
+
+        size_rows = ps.tile([P, PACK, P], F32, name="size_rows")
+        for j in range(PACK):
+            nc.tensor.transpose(size_rows[:, j, :], size4[:, j : j + 1].to_broadcast([P, P]), ident[:])
+
+        neg_max = sb.tile([P, 1], F32, name="neg_max", tag="got1", align_bytes=64)
+        nc.vector.tensor_reduce(neg_max[:], scores[:], mybir.AxisListType.X, ALU.max, negate=True)
+        row_max = sb.tile([P, 1], F32, name="row_max")
+        nc.vector.tensor_scalar(row_max[:], neg_max[:], -1.0, None, ALU.mult)
+        got0 = sb.tile([P, I], BF16, name="got0", align_bytes=64)
+        nc.scalar.activation(got0[:], pools[0][:].indirect(offsets[:]), ACT.Copy)
+        p = sb.tile([P, I], F32, name="p", tag="pool0", align_bytes=64)
+        z = sb.tile([P, 1], F32, name="z")
+        nc.scalar.activation(p[:], scores[:], ACT.Exp, bias=neg_max[:], scale=1.0, accum_out=z[:])
+        inv_z = sb.tile([P, 1], F32, name="inv_z")
+        nc.vector.reciprocal(inv_z[:], z[:])
+        pb = sb.tile([P, I], F32, name="pb")
+        pb_sum = sb.tile([P, 1], F32, name="pb_sum", tag="column")
+        nc.vector.scalar_tensor_tensor(pb[:], scores[:], row_max[:], p[:], ALU.subtract, ALU.mult, accum_out=pb_sum[:])
+        neg_inv_z = sb.tile([P, 1], F32, name="neg_inv_z")
+        nc.vector.tensor_scalar(neg_inv_z[:], inv_z[:], -1.0, None, ALU.mult)
+        w_bf = sb.tile([P, I], BF16, name="w_bf", align_bytes=64)
+        nc.vector.scalar_tensor_tensor(
+            w_bf[:].rearrange("p (n j) -> p n j", j=PACK), p[:].rearrange("p (n j) -> p n j", j=PACK), inv_z[:],
+            size_rows[:].rearrange("p j n -> p n j"), ALU.mult, ALU.mult,
+        )
+
+        def turn_and_quantise(rows_bf, name, bank_tag, copy):
+            words = rows_bf[:].bitcast(F32)
+            turned = ps.tile([P, 2, P], F32, name=name + "_turned", tag=bank_tag)
+            for u in range(2):
+                nc.tensor.transpose(turned[:, u, :], words[:, u : I // 2 : 2], ident[:])
+            grouped = sb.tile([P, P * PACK], BF16, name=name + "_grouped", tag=name + "_grouped", align_bytes=64)
+            copy(grouped[:].bitcast(F32).rearrange("p (r u) -> p r u", u=2), turned[:].rearrange("p u r -> p r u"))
+            codes = sb.tile([P, P], U32, name=name + "_codes", align_bytes=64)
+            plane = sb.tile([P, P], U8, name=name + "_plane", align_bytes=64)
+            nc.vector.quantize_mx(out=codes[:].bitcast(FP8X4), scales=plane[:], in_=grouped[:])
+            return codes, plane
+
+        w_codes, w_plane = turn_and_quantise(w_bf, "w", "turn_w", nc.vector.tensor_copy)
+
+        def gather_on_scalar(j, tag):
+            got = sb.tile([P, I], BF16, name="got%d" % j, tag=tag, align_bytes=64)
+            nc.scalar.activation(got[:], pools[j][:].indirect(offsets[:]), ACT.Copy)
+            return got
+
+        last = BLOCKS - 1
+        quantised = [turn_and_quantise(got0, "v0", "turn0", nc.vector.tensor_copy)]
+        quantised.append(turn_and_quantise(gather_on_scalar(1, "got1"), "v1", "turn1", nc.vector.tensor_copy))
+        th_in = sb.tile([P, 1], F32, name="th_in")
+        nc.gpsimd.tensor_scalar(th_in[:], th_col[:], EN_MAX, 0.0, ALU.min, ALU.max)
+        neg_th_in = sb.tile([P, 1], F32, name="neg_th_in")
+        nc.gpsimd.tensor_scalar(neg_th_in[:], th_in[:], -1.0, 0.0, ALU.mult, ALU.add)
+        th_out = sb.tile([P, 1], F32, name="th_out")
+        nc.gpsimd.tensor_scalar(th_out[:], th_col[:], neg_th_in[:], steep_col[:], ALU.add, ALU.mult)
+        base_by_z = sb.tile([P, 1], F32, name="base_by_z", tag="pool1", align_bytes=64)
+        nc.scalar.activation(base_by_z[:], pb_sum[:], ACT.Exp, scale=neg_inv_z[:], bias=neg_th_in[:])
+        base = sb.tile([P, 1], F32, name="base")
+        nc.scalar.activation(base[:], base_by_z[:], ACT.Copy, scale=z[:])
+        outer = sb.tile([P, 1], F32, name="outer", tag="column")
+        nc.scalar.activation(outer[:], th_out[:], ACT.Exp, scale=-1.0)
+        inner = sb.tile([P, 1], F32, name="inner")
+        nc.gpsimd.tensor_tensor(inner[:], base[:], steep_col[:], ALU.pow)
+        odds1 = sb.tile([P, 1], F32, name="odds1")
+        nc.vector.tensor_scalar(odds1[:], inner[:], outer[:], 1.0, ALU.mult, ALU.add)
+        gate = sb.tile([P, 1], F32, name="gate")
+        nc.vector.reciprocal(gate[:], odds1[:])
+        rest = sb.tile([P, 1], F32, name="rest")
+        nc.vector.tensor_scalar(rest[:], gate[:], -1.0, 1.0, ALU.mult, ALU.add)
+
+        quantised.append(turn_and_quantise(gather_on_scalar(2, "pool1"), "v2", "turn2", nc.vector.tensor_copy))
+        stand_rows = ps.tile([P, PACK, P], F32, name="stand_rows", tag="turn1")
+        for j in range(PACK):
+            nc.tensor.transpose(stand_rows[:, j, :], stand4[:, j : j + 1].to_broadcast([P, P]), ident[:])
+        standing = sb.tile([P, E], F32, name="standing", tag="pool2", align_bytes=64)
+        nc.scalar.activation(
+            standing[:].rearrange("p (n j) -> p n j", j=PACK), stand_rows[:].rearrange("p j n -> p n j"),
+            ACT.Copy, scale=rest[:],
+        )
+
+        def finish(read, cols, name, tag):
+            result = sb.tile([P, cols.stop - cols.start], F32, name=name, tag=tag, align_bytes=64)
+            nc.vector.scalar_tensor_tensor(result[:], read, gate[:], standing[:, cols], ALU.mult, ALU.add)
+            nc.sync.dma_start(out[:, cols], result[:])
+
+        def multiply(read, operand):
+            v_codes, v_plane = operand
+            nc.tensor.matmul_mx(
+                out=read, lhsT=w_codes[:].bitcast(FP8X4), lhsT_scale=w_plane[:],
+                rhs=v_codes[:].bitcast(FP8X4), rhs_scale=v_plane[:], start=True, stop=True,
+            )
+
+
+        read_early = ps.tile([P, last * P], F32, name="read_early", tag="turn2")
+        for b in range(last):
+            multiply(read_early[:, b * P : (b + 1) * P], quantised[b])
+        got = sb.tile([P, I], BF16, name="got_last", tag="v2_grouped", align_bytes=64)
+        nc.vector.tensor_copy(got[:, :SPLIT], pools[last][:].indirect(offsets[:, : SPLIT // 16]))
+        nc.scalar.activation(got[:, SPLIT:], pools[last][:].indirect(offsets[:, SPLIT // 16 :]), ACT.Copy)
+        read_last = ps.tile([P, P], F32, name="read_last")
+        multiply(read_last[:], turn_and_quantise(got, "v3", "turn3", nc.vector.tensor_copy))
+        finish(read_early[:], slice(0, last * P), "result_early", "pool3")
+        finish(read_last[:], slice(last * P, E), "result_last", "result_last")

@@ -21,7 +21,7 @@ ACT = mybir.ActivationFunctionType
 P = 128
 PACK = 4
 BLOCKS = E // P
-SPLIT = 288
+SPLIT = 256
 EN_MAX = math.log(I)
 
 
@@ -51,13 +51,13 @@ def tile_attend_certaintyread_kernel(tc, query, keys_words, keys_scales, th, ste
         q_raw = sb.tile([P, PACK, Q], F32, name="q_raw", align_bytes=64)
         nc.sync.dma_start(offsets[:], offs)
         nc.sync.dma_start(key_words[:].bitcast(I32), keys_words[0].bitcast(I32))
+        nc.sync.dma_start(q_raw[:], query.rearrange("(p j) q -> p j q", j=PACK))
         nc.sync.dma_start(size4[:], size.rearrange("o (p j) -> p (o j)", j=PACK))
         for quad in range(4):
             nc.sync.dma_start(
                 key_bytes[32 * quad : 32 * quad + 4, :].bitcast(I32),
                 keys_scales[0, 4 * quad : 4 * quad + 4, :].bitcast(I32),
             )
-        nc.sync.dma_start(q_raw[:], query.rearrange("(p j) q -> p j q", j=PACK))
         pools = [load_pool(0)]
         with nc.allow_non_contiguous_dma(reason="one value a partition"):
             nc.sync.dma_start(th_col[:], th)
@@ -95,25 +95,23 @@ def tile_attend_certaintyread_kernel(tc, query, keys_words, keys_scales, th, ste
         p = sb.tile([P, I], F32, name="p", tag="pool0", align_bytes=64)
         z = sb.tile([P, 1], F32, name="z")
         nc.scalar.activation(p[:], scores[:], ACT.Exp, bias=neg_max[:], scale=1.0, accum_out=z[:])
+        pb = sb.tile([P, I], F32, name="pb")
+        pb_sum = sb.tile([P, 1], F32, name="pb_sum", tag="got2", align_bytes=64)
+        nc.vector.scalar_tensor_tensor(pb[:], scores[:], row_max[:], p[:], ALU.subtract, ALU.mult, accum_out=pb_sum[:])
         inv_z = sb.tile([P, 1], F32, name="inv_z")
         nc.vector.reciprocal(inv_z[:], z[:])
-        pb = sb.tile([P, I], F32, name="pb")
-        pb_sum = sb.tile([P, 1], F32, name="pb_sum", tag="column")
-        nc.vector.scalar_tensor_tensor(pb[:], scores[:], row_max[:], p[:], ALU.subtract, ALU.mult, accum_out=pb_sum[:])
-        neg_inv_z = sb.tile([P, 1], F32, name="neg_inv_z")
-        nc.vector.tensor_scalar(neg_inv_z[:], inv_z[:], -1.0, None, ALU.mult)
         w_bf = sb.tile([P, I], BF16, name="w_bf", align_bytes=64)
         nc.vector.scalar_tensor_tensor(
             w_bf[:].rearrange("p (n j) -> p n j", j=PACK), p[:].rearrange("p (n j) -> p n j", j=PACK), inv_z[:],
             size_rows[:].rearrange("p j n -> p n j"), ALU.mult, ALU.mult,
         )
 
-        def turn_and_quantise(rows_bf, name, bank_tag, copy):
+        def turn_and_quantise(rows_bf, name, bank_tag, copy, grouped_tag=None):
             words = rows_bf[:].bitcast(F32)
             turned = ps.tile([P, 2, P], F32, name=name + "_turned", tag=bank_tag)
             for u in range(2):
                 nc.tensor.transpose(turned[:, u, :], words[:, u : I // 2 : 2], ident[:])
-            grouped = sb.tile([P, P * PACK], BF16, name=name + "_grouped", tag=name + "_grouped", align_bytes=64)
+            grouped = sb.tile([P, P * PACK], BF16, name=name + "_grouped", tag=grouped_tag or name + "_grouped", align_bytes=64)
             copy(grouped[:].bitcast(F32).rearrange("p (r u) -> p r u", u=2), turned[:].rearrange("p u r -> p r u"))
             codes = sb.tile([P, P], U32, name=name + "_codes", align_bytes=64)
             plane = sb.tile([P, P], U8, name=name + "_plane", align_bytes=64)
@@ -130,36 +128,35 @@ def tile_attend_certaintyread_kernel(tc, query, keys_words, keys_scales, th, ste
         last = BLOCKS - 1
         quantised = [turn_and_quantise(got0, "v0", "turn0", nc.vector.tensor_copy)]
         quantised.append(turn_and_quantise(gather_on_scalar(1, "got1"), "v1", "turn1", nc.vector.tensor_copy))
-        th_in = sb.tile([P, 1], F32, name="th_in")
-        nc.gpsimd.tensor_scalar(th_in[:], th_col[:], EN_MAX, 0.0, ALU.min, ALU.max)
-        neg_th_in = sb.tile([P, 1], F32, name="neg_th_in")
-        nc.gpsimd.tensor_scalar(neg_th_in[:], th_in[:], -1.0, 0.0, ALU.mult, ALU.add)
-        th_out = sb.tile([P, 1], F32, name="th_out")
-        nc.gpsimd.tensor_scalar(th_out[:], th_col[:], neg_th_in[:], steep_col[:], ALU.add, ALU.mult)
-        base_by_z = sb.tile([P, 1], F32, name="base_by_z", tag="pool1", align_bytes=64)
-        nc.scalar.activation(base_by_z[:], pb_sum[:], ACT.Exp, scale=neg_inv_z[:], bias=neg_th_in[:])
-        base = sb.tile([P, 1], F32, name="base")
-        nc.scalar.activation(base[:], base_by_z[:], ACT.Copy, scale=z[:])
-        outer = sb.tile([P, 1], F32, name="outer", tag="column")
-        nc.scalar.activation(outer[:], th_out[:], ACT.Exp, scale=-1.0)
-        inner = sb.tile([P, 1], F32, name="inner")
-        nc.gpsimd.tensor_tensor(inner[:], base[:], steep_col[:], ALU.pow)
-        odds1 = sb.tile([P, 1], F32, name="odds1")
-        nc.vector.tensor_scalar(odds1[:], inner[:], outer[:], 1.0, ALU.mult, ALU.add)
-        gate = sb.tile([P, 1], F32, name="gate")
-        nc.vector.reciprocal(gate[:], odds1[:])
-        rest = sb.tile([P, 1], F32, name="rest")
-        nc.vector.tensor_scalar(rest[:], gate[:], -1.0, 1.0, ALU.mult, ALU.add)
 
-        quantised.append(turn_and_quantise(gather_on_scalar(2, "pool1"), "v2", "turn2", nc.vector.tensor_copy))
-        stand_rows = ps.tile([P, PACK, P], F32, name="stand_rows", tag="turn1")
+        def column(name):
+            return sb.tile([P, 1], F32, name=name)
+
+        minus_one, euler = column("minus_one"), column("euler")
+        nc.gpsimd.memset(minus_one[:], -1.0)
+        nc.gpsimd.tensor_scalar(euler[:], minus_one[:], -math.e, 0.0, ALU.mult, ALU.add)
+        th_in, th_out, outer, neg_steep = column("th_in"), column("th_out"), column("outer"), column("neg_steep")
+        nc.gpsimd.tensor_scalar(th_in[:], th_col[:], EN_MAX, 0.0, ALU.min, ALU.max)
+        nc.gpsimd.tensor_scalar(th_out[:], th_in[:], th_col[:], steep_col[:], ALU.subtract, ALU.mult)
+        nc.gpsimd.tensor_scalar(neg_steep[:], steep_col[:], -1.0, 0.0, ALU.mult, ALU.add)
+        nc.gpsimd.tensor_tensor(outer[:], euler[:], th_out[:], ALU.pow)
+        base_z = sb.tile([P, 1], F32, name="base_z", tag="pool1", align_bytes=64)
+        nc.scalar.activation(base_z[:], pb_sum[:], ACT.Exp, scale=inv_z[:], bias=th_in[:])
+        base, inner, odds1, gate, rest = column("base"), column("inner"), column("odds1"), column("gate"), column("rest")
+        nc.gpsimd.tensor_tensor(base[:], base_z[:], inv_z[:], ALU.mult)
+        nc.gpsimd.tensor_tensor(inner[:], base[:], neg_steep[:], ALU.pow)
+        nc.gpsimd.tensor_scalar(odds1[:], inner[:], outer[:], 1.0, ALU.mult, ALU.add)
+        nc.gpsimd.tensor_tensor(gate[:], odds1[:], minus_one[:], ALU.pow)
+        nc.gpsimd.tensor_scalar(rest[:], gate[:], -1.0, 1.0, ALU.mult, ALU.add)
+
+        got2 = gather_on_scalar(2, "got2")
+        got = sb.tile([P, I], BF16, name="got_last", tag="v1_grouped", align_bytes=64)
+        nc.vector.tensor_copy(got[:, :SPLIT], pools[last][:].indirect(offsets[:, : SPLIT // 16]))
+        nc.scalar.activation(got[:, SPLIT:], pools[last][:].indirect(offsets[:, SPLIT // 16 :]), ACT.Copy)
+        quantised.append(turn_and_quantise(got2, "v2", "turn2", nc.vector.tensor_copy, "pool3"))
+        stand_rows = ps.tile([P, PACK, P], F32, name="stand_rows", tag="scores")
         for j in range(PACK):
             nc.tensor.transpose(stand_rows[:, j, :], stand4[:, j : j + 1].to_broadcast([P, P]), ident[:])
-        standing = sb.tile([P, E], F32, name="standing", tag="pool2", align_bytes=64)
-        nc.scalar.activation(
-            standing[:].rearrange("p (n j) -> p n j", j=PACK), stand_rows[:].rearrange("p j n -> p n j"),
-            ACT.Copy, scale=rest[:],
-        )
 
         def finish(read, cols, name, tag):
             result = sb.tile([P, cols.stop - cols.start], F32, name=name, tag=tag, align_bytes=64)
@@ -177,10 +174,13 @@ def tile_attend_certaintyread_kernel(tc, query, keys_words, keys_scales, th, ste
         read_early = ps.tile([P, last * P], F32, name="read_early", tag="turn2")
         for b in range(last):
             multiply(read_early[:, b * P : (b + 1) * P], quantised[b])
-        got = sb.tile([P, I], BF16, name="got_last", tag="v2_grouped", align_bytes=64)
-        nc.vector.tensor_copy(got[:, :SPLIT], pools[last][:].indirect(offsets[:, : SPLIT // 16]))
-        nc.scalar.activation(got[:, SPLIT:], pools[last][:].indirect(offsets[:, SPLIT // 16 :]), ACT.Copy)
         read_last = ps.tile([P, P], F32, name="read_last")
         multiply(read_last[:], turn_and_quantise(got, "v3", "turn3", nc.vector.tensor_copy))
-        finish(read_early[:], slice(0, last * P), "result_early", "pool3")
+        standing = sb.tile([P, E], F32, name="standing", tag="pool3", align_bytes=64)
+        nc.scalar.activation(
+            standing[:].rearrange("p (n j) -> p n j", j=PACK), stand_rows[:].rearrange("p j n -> p n j"),
+            ACT.Copy, scale=rest[:],
+        )
+
+        finish(read_early[:], slice(0, last * P), "result_early", "v3_grouped")
         finish(read_last[:], slice(last * P, E), "result_last", "result_last")

@@ -21,7 +21,7 @@ ACT = mybir.ActivationFunctionType
 P = 128
 PACK = 4
 BLOCKS = E // P
-SPLIT = 256
+SPLIT = 288
 EN_MAX = math.log(I)
 
 
@@ -58,12 +58,11 @@ def tile_attend_certaintyread_kernel(tc, query, keys_words, keys_scales, th, ste
                 key_bytes[32 * quad : 32 * quad + 4, :].bitcast(I32),
                 keys_scales[0, 4 * quad : 4 * quad + 4, :].bitcast(I32),
             )
-        pools = [load_pool(0)]
+        pools = [load_pool(j) for j in range(BLOCKS)]
         with nc.allow_non_contiguous_dma(reason="one value a partition"):
-            nc.sync.dma_start(th_col[:], th)
-            nc.sync.dma_start(steep_col[:], steep)
-        nc.sync.dma_start(stand4[:], stand.rearrange("o (p j) -> p (o j)", j=PACK))
-        pools.extend(load_pool(j) for j in range(1, BLOCKS))
+            nc.gpsimd.dma_start(th_col[:], th)
+            nc.gpsimd.dma_start(steep_col[:], steep)
+        nc.gpsimd.dma_start(stand4[:], stand.rearrange("o (p j) -> p (o j)", j=PACK))
 
         got_words = sb.tile([P, I], U16, name="got_words", align_bytes=64)
         got_bytes = sb.tile([P, I], U8, name="got_bytes", align_bytes=64)
@@ -176,7 +175,7 @@ def tile_attend_certaintyread_kernel(tc, query, keys_words, keys_scales, th, ste
             multiply(read_early[:, b * P : (b + 1) * P], quantised[b])
         read_last = ps.tile([P, P], F32, name="read_last")
         multiply(read_last[:], turn_and_quantise(got, "v3", "turn3", nc.vector.tensor_copy))
-        standing = sb.tile([P, E], F32, name="standing", tag="pool3", align_bytes=64)
+        standing = sb.tile([P, E], F32, name="standing", tag="v1_grouped", align_bytes=64)
         nc.scalar.activation(
             standing[:].rearrange("p (n j) -> p n j", j=PACK), stand_rows[:].rearrange("p j n -> p n j"),
             ACT.Copy, scale=rest[:],

@@ -29,6 +29,7 @@ def tile_attend_certaintyread_kernel(tc, query, keys_words, keys_scales, th, ste
     nc = tc.nc
     with ExitStack() as ctx:
         sb = ctx.enter_context(tc.tile_pool(name="sb", bufs=1))
+        tail = ctx.enter_context(tc.tile_pool(name="tail", bufs=1))
         ps = ctx.enter_context(tc.psum_pool(name="ps", bufs=1))
 
         offsets = sb.tile([P, I // 16], U16, name="offsets")
@@ -40,7 +41,10 @@ def tile_attend_certaintyread_kernel(tc, query, keys_words, keys_scales, th, ste
         make_identity(nc, ident[:])
 
         def load_pool(j):
-            pool = sb.tile([P, T], F32, name="pool%d" % j, tag="pool%d" % j, align_bytes=64)
+            if j == BLOCKS - 1:
+                pool = tail.tile([P, T], F32, name="pool_last", align_bytes=64, offset=0)
+            else:
+                pool = sb.tile([P, T], F32, name="pool%d" % j, tag="pool%d" % j, align_bytes=64)
             nc.sync.dma_start(pool[:], vals[j * P : (j + 1) * P, :])
             return pool
 
@@ -105,12 +109,13 @@ def tile_attend_certaintyread_kernel(tc, query, keys_words, keys_scales, th, ste
             size_rows[:].rearrange("p j n -> p n j"), ALU.mult, ALU.mult,
         )
 
-        def turn_and_quantise(rows_bf, name, bank_tag, copy, grouped_tag=None):
+        def turn_and_quantise(rows_bf, name, bank_tag, copy, grouped=None):
             words = rows_bf[:].bitcast(F32)
             turned = ps.tile([P, 2, P], F32, name=name + "_turned", tag=bank_tag)
             for u in range(2):
                 nc.tensor.transpose(turned[:, u, :], words[:, u : I // 2 : 2], ident[:])
-            grouped = sb.tile([P, P * PACK], BF16, name=name + "_grouped", tag=grouped_tag or name + "_grouped", align_bytes=64)
+            if grouped is None:
+                grouped = sb.tile([P, P * PACK], BF16, name=name + "_grouped", tag=name + "_grouped", align_bytes=64)
             copy(grouped[:].bitcast(F32).rearrange("p (r u) -> p r u", u=2), turned[:].rearrange("p u r -> p r u"))
             codes = sb.tile([P, P], U32, name=name + "_codes", align_bytes=64)
             plane = sb.tile([P, P], U8, name=name + "_plane", align_bytes=64)
@@ -152,10 +157,16 @@ def tile_attend_certaintyread_kernel(tc, query, keys_words, keys_scales, th, ste
         got = sb.tile([P, I], BF16, name="got_last", tag="v1_grouped", align_bytes=64)
         nc.vector.tensor_copy(got[:, :SPLIT], pools[last][:].indirect(offsets[:, : SPLIT // 16]))
         nc.scalar.activation(got[:, SPLIT:], pools[last][:].indirect(offsets[:, SPLIT // 16 :]), ACT.Copy)
-        quantised.append(turn_and_quantise(got2, "v2", "turn2", nc.vector.tensor_copy, "pool3"))
+        grouped2 = tail.tile([P, P * PACK], BF16, name="v2_grouped", align_bytes=64, offset=0)
+        quantised.append(turn_and_quantise(got2, "v2", "turn2", nc.vector.tensor_copy, grouped2))
         stand_rows = ps.tile([P, PACK, P], F32, name="stand_rows", tag="scores")
         for j in range(PACK):
             nc.tensor.transpose(stand_rows[:, j, :], stand4[:, j : j + 1].to_broadcast([P, P]), ident[:])
+        standing = tail.tile([P, E], F32, name="standing", align_bytes=64, offset=2 * P * PACK)
+        nc.scalar.activation(
+            standing[:].rearrange("p (n j) -> p n j", j=PACK), stand_rows[:].rearrange("p j n -> p n j"),
+            ACT.Copy, scale=rest[:],
+        )
 
         def finish(read, cols, name, tag):
             result = sb.tile([P, cols.stop - cols.start], F32, name=name, tag=tag, align_bytes=64)
@@ -174,12 +185,6 @@ def tile_attend_certaintyread_kernel(tc, query, keys_words, keys_scales, th, ste
         for b in range(last):
             multiply(read_early[:, b * P : (b + 1) * P], quantised[b])
         read_last = ps.tile([P, P], F32, name="read_last")
-        multiply(read_last[:], turn_and_quantise(got, "v3", "turn3", nc.vector.tensor_copy))
-        standing = sb.tile([P, E], F32, name="standing", tag="v1_grouped", align_bytes=64)
-        nc.scalar.activation(
-            standing[:].rearrange("p (n j) -> p n j", j=PACK), stand_rows[:].rearrange("p j n -> p n j"),
-            ACT.Copy, scale=rest[:],
-        )
-
+        multiply(read_last[:], turn_and_quantise(got, "v3", "turn3", nc.scalar.copy))
         finish(read_early[:], slice(0, last * P), "result_early", "v3_grouped")
         finish(read_last[:], slice(last * P, E), "result_last", "result_last")

import math
from contextlib import ExitStack

import concourse.mybir as mybir
from concourse.masks import make_identity

D, T, I, Q, E = 512, 2048, 512, 128, 512
FLOPS = 2 * Q * D * I + 2 * Q * I * E

F32 = mybir.dt.float32
BF16 = mybir.dt.bfloat16
I32 = mybir.dt.int32
U32 = mybir.dt.uint32
U16 = mybir.dt.uint16
U8 = mybir.dt.uint8
FP8X4 = mybir.dt.float8_e4m3fn_x4
FP4X4 = mybir.dt.float4_e2m1fn_x4
ALU = mybir.AluOpType
ACT = mybir.ActivationFunctionType

P = 128
PACK = 4
BLOCKS = E // P
SPLIT = 288
EN_MAX = math.log(I)


def tile_attend_certaintyread_kernel(tc, query, keys_words, keys_scales, th, steep, stand, size, vals, offs, out):
    nc = tc.nc
    with ExitStack() as ctx:
        sb = ctx.enter_context(tc.tile_pool(name="sb", bufs=1))
        tail = ctx.enter_context(tc.tile_pool(name="tail", bufs=1))
        ps = ctx.enter_context(tc.psum_pool(name="ps", bufs=1))

        offsets = sb.tile([P, I // 16], U16, name="offsets")
        key_words = sb.tile([P, T], U16, name="key_words", align_bytes=64)
        key_bytes = sb.tile([P, T], U8, name="key_bytes", align_bytes=64)
        ident = sb.tile([P, P], F32, name="ident")

        nc.vector.memset(key_bytes[:].bitcast(I32), 0)
        make_identity(nc, ident[:])

        def load_pool(j):
            if j == BLOCKS - 1:
                pool = tail.tile([P, T], F32, name="pool_last", align_bytes=64, offset=0)
            else:
                pool = sb.tile([P, T], F32, name="pool%d" % j, tag="pool%d" % j, align_bytes=64)
            nc.sync.dma_start(pool[:], vals[j * P : (j + 1) * P, :])
            return pool

        size4 = sb.tile([P, PACK], F32, name="size4")
        stand4 = sb.tile([P, PACK], F32, name="stand4")
        th_col = sb.tile([P, 1], F32, name="th_col")
        steep_col = sb.tile([P, 1], F32, name="steep_col")
        q_raw = sb.tile([P, PACK, Q], F32, name="q_raw", align_bytes=64)
        nc.sync.dma_start(offsets[:], offs)
        nc.sync.dma_start(key_words[:].bitcast(I32), keys_words[0].bitcast(I32))
        nc.sync.dma_start(q_raw[:], query.rearrange("(p j) q -> p j q", j=PACK))
        nc.sync.dma_start(size4[:], size.rearrange("o (p j) -> p (o j)", j=PACK))
        for quad in range(4):
            nc.sync.dma_start(
                key_bytes[32 * quad : 32 * quad + 4, :].bitcast(I32),
                keys_scales[0, 4 * quad : 4 * quad + 4, :].bitcast(I32),
            )
        pools = [load_pool(j) for j in range(BLOCKS)]
        with nc.allow_non_contiguous_dma(reason="one value a partition"):
            nc.gpsimd.dma_start(th_col[:], th)
            nc.gpsimd.dma_start(steep_col[:], steep)
        nc.gpsimd.dma_start(stand4[:], stand.rearrange("o (p j) -> p (o j)", j=PACK))

        got_words = sb.tile([P, I], U16, name="got_words", align_bytes=64)
        got_bytes = sb.tile([P, I], U8, name="got_bytes", align_bytes=64)
        nc.vector.tensor_copy(got_words[:], key_words[:].indirect(offsets[:]))
        nc.vector.tensor_copy(got_bytes[:], key_bytes[:].indirect(offsets[:]))

        q_bf = sb.tile([P, Q * PACK], BF16, name="q_bf", align_bytes=64)
        nc.scalar.copy(q_bf[:].rearrange("p (q j) -> p q j", j=PACK), q_raw[:].rearrange("p j q -> p q j"))
        q_codes = sb.tile([P, Q], U32, name="q_codes", align_bytes=64)
        q_plane = sb.tile([P, Q], U8, name="q_plane", align_bytes=64)
        nc.vector.quantize_mx(out=q_codes[:].bitcast(FP8X4), scales=q_plane[:], in_=q_bf[:])

        scores = ps.tile([P, I], F32, name="scores", tag="scores")
        nc.tensor.matmul_mx(
            out=scores[:], lhsT=q_codes[:].bitcast(FP8X4), lhsT_scale=q_plane[:],
            rhs=got_words[:].bitcast(FP4X4), rhs_scale=got_bytes[:], start=True, stop=True,
        )

        size_rows = ps.tile([P, PACK, P], F32, name="size_rows")
        for j in range(PACK):
            nc.tensor.transpose(size_rows[:, j, :], size4[:, j : j + 1].to_broadcast([P, P]), ident[:])

        neg_max = sb.tile([P, 1], F32, name="neg_max", tag="got1", align_bytes=64)
        nc.vector.tensor_reduce(neg_max[:], scores[:], mybir.AxisListType.X, ALU.max, negate=True)
        row_max = sb.tile([P, 1], F32, name="row_max")
        nc.vector.tensor_scalar(row_max[:], neg_max[:], -1.0, None, ALU.mult)
        got0 = sb.tile([P, I], BF16, name="got0", align_bytes=64)
        nc.scalar.activation(got0[:], pools[0][:].indirect(offsets[:]), ACT.Copy)
        p = sb.tile([P, I], F32, name="p", tag="pool0", align_bytes=64)
        z = sb.tile([P, 1], F32, name="z")
        nc.scalar.activation(p[:], scores[:], ACT.Exp, bias=neg_max[:], scale=1.0, accum_out=z[:])
        pb = sb.tile([P, I], F32, name="pb")
        pb_sum = sb.tile([P, 1], F32, name="pb_sum", tag="got2", align_bytes=64)
        nc.vector.scalar_tensor_tensor(pb[:], scores[:], row_max[:], p[:], ALU.subtract, ALU.mult, accum_out=pb_sum[:])
        inv_z = sb.tile([P, 1], F32, name="inv_z")
        nc.vector.reciprocal(inv_z[:], z[:])
        w_bf = sb.tile([P, I], BF16, name="w_bf", align_bytes=64)
        nc.vector.scalar_tensor_tensor(
            w_bf[:].rearrange("p (n j) -> p n j", j=PACK), p[:].rearrange("p (n j) -> p n j", j=PACK), inv_z[:],
            size_rows[:].rearrange("p j n -> p n j"), ALU.mult, ALU.mult,
        )

        def turn_and_quantise(rows_bf, name, bank_tag, copy, grouped=None):
            words = rows_bf[:].bitcast(F32)
            turned = ps.tile([P, 2, P], F32, name=name + "_turned", tag=bank_tag)
            for u in range(2):
                nc.tensor.transpose(turned[:, u, :], words[:, u : I // 2 : 2], ident[:])
            if grouped is None:
                grouped = sb.tile([P, P * PACK], BF16, name=name + "_grouped", tag=name + "_grouped", align_bytes=64)
            copy(grouped[:].bitcast(F32).rearrange("p (r u) -> p r u", u=2), turned[:].rearrange("p u r -> p r u"))
            codes = sb.tile([P, P], U32, name=name + "_codes", align_bytes=64)
            plane = sb.tile([P, P], U8, name=name + "_plane", align_bytes=64)
            nc.vector.quantize_mx(out=codes[:].bitcast(FP8X4), scales=plane[:], in_=grouped[:])
            return codes, plane

        w_codes, w_plane = turn_and_quantise(w_bf, "w", "turn_w", nc.vector.tensor_copy)

        def gather_on_scalar(j, tag):
            got = sb.tile([P, I], BF16, name="got%d" % j, tag=tag, align_bytes=64)
            nc.scalar.activation(got[:], pools[j][:].indirect(offsets[:]), ACT.Copy)
            return got

        last = BLOCKS - 1
        quantised = [turn_and_quantise(got0, "v0", "turn0", nc.vector.tensor_copy)]
        quantised.append(turn_and_quantise(gather_on_scalar(1, "got1"), "v1", "turn1", nc.vector.tensor_copy))

        def column(name):
            return sb.tile([P, 1], F32, name=name)

        minus_one, euler = column("minus_one"), column("euler")
        nc.gpsimd.memset(minus_one[:], -1.0)
        nc.gpsimd.tensor_scalar(euler[:], minus_one[:], -math.e, 0.0, ALU.mult, ALU.add)
        th_in, th_out, outer, neg_steep = column("th_in"), column("th_out"), column("outer"), column("neg_steep")
        nc.gpsimd.tensor_scalar(th_in[:], th_col[:], EN_MAX, 0.0, ALU.min, ALU.max)
        nc.gpsimd.tensor_scalar(th_out[:], th_in[:], th_col[:], steep_col[:], ALU.subtract, ALU.mult)
        nc.gpsimd.tensor_scalar(neg_steep[:], steep_col[:], -1.0, 0.0, ALU.mult, ALU.add)
        nc.gpsimd.tensor_tensor(outer[:], euler[:], th_out[:], ALU.pow)
        base_z = sb.tile([P, 1], F32, name="base_z", tag="pool1", align_bytes=64)
        nc.scalar.activation(base_z[:], pb_sum[:], ACT.Exp, scale=inv_z[:], bias=th_in[:])
        base, inner, odds1, gate, rest = column("base"), column("inner"), column("odds1"), column("gate"), column("rest")
        nc.gpsimd.tensor_tensor(base[:], base_z[:], inv_z[:], ALU.mult)
        nc.gpsimd.tensor_tensor(inner[:], base[:], neg_steep[:], ALU.pow)
        nc.gpsimd.tensor_scalar(odds1[:], inner[:], outer[:], 1.0, ALU.mult, ALU.add)
        nc.gpsimd.tensor_tensor(gate[:], odds1[:], minus_one[:], ALU.pow)
        nc.gpsimd.tensor_scalar(rest[:], gate[:], -1.0, 1.0, ALU.mult, ALU.add)

        got2 = gather_on_scalar(2, "got2")
        got = sb.tile([P, I], BF16, name="got_last", tag="v1_grouped", align_bytes=64)
        nc.vector.tensor_copy(got[:, :SPLIT], pools[last][:].indirect(offsets[:, : SPLIT // 16]))
        nc.scalar.activation(got[:, SPLIT:], pools[last][:].indirect(offsets[:, SPLIT // 16 :]), ACT.Copy)
        grouped2 = tail.tile([P, P * PACK], BF16, name="v2_grouped", align_bytes=64, offset=0)
        quantised.append(turn_and_quantise(got2, "v2", "turn2", nc.vector.tensor_copy, grouped2))
        stand_rows = ps.tile([P, PACK, P], F32, name="stand_rows", tag="scores")
        for j in range(PACK):
            nc.tensor.transpose(stand_rows[:, j, :], stand4[:, j : j + 1].to_broadcast([P, P]), ident[:])
        standing = tail.tile([P, E], F32, name="standing", align_bytes=64, offset=2 * P * PACK)
        nc.scalar.activation(
            standing[:].rearrange("p (n j) -> p n j", j=PACK), stand_rows[:].rearrange("p j n -> p n j"),
            ACT.Copy, scale=rest[:],
        )

        def finish(read, cols, name, tag):
            result = sb.tile([P, cols.stop - cols.start], F32, name=name, tag=tag, align_bytes=64)
            nc.vector.scalar_tensor_tensor(result[:], read, gate[:], standing[:, cols], ALU.mult, ALU.add)
            nc.sync.dma_start(out[:, cols], result[:])

        def multiply(read, operand):
            v_codes, v_plane = operand
            nc.tensor.matmul_mx(
                out=read, lhsT=w_codes[:].bitcast(FP8X4), lhsT_scale=w_plane[:],
                rhs=v_codes[:].bitcast(FP8X4), rhs_scale=v_plane[:], start=True, stop=True,
            )


        read_early = ps.tile([P, last * P], F32, name="read_early", tag="turn2")
        for b in range(last):
            multiply(read_early[:, b * P : (b + 1) * P], quantised[b])
        read_last = ps.tile([P, P], F32, name="read_last")
        multiply(read_last[:], turn_and_quantise(got, "v3", "turn3", nc.scalar.copy))
        finish(read_early[:], slice(0, last * P), "result_early", "v3_grouped")
        finish(read_last[:], slice(last * P, E), "result_last", "result_last")
